import numpy as np
CORES = [16,17,18,19,150,151]
N = 6
R, T = 8192, 2048
HOST = [c // 128 for c in CORES]
G = [[r for r in range(N) if HOST[r] == h] for h in sorted(set(HOST))]
H = len(G); K = [sorted(set(HOST)).index(h) for h in HOST]
def entries(a): return a.T.reshape(-1)
def pack(v, P): return np.ascontiguousarray(np.asarray(v, np.int32).reshape(-1, P).T)
def among(rng, a): return rng.permutation(np.concatenate([a, rng.choice(a, T - len(a))]))
def lists(rng, how):
    O = np.stack([among(rng, np.arange(N)) for g in G])
    if how == "away": O = np.stack([among(rng, [r for r in range(N) if r not in g]) for g in G])
    if how == "home": O = np.stack([among(rng, g) for g in G])
    J = rng.integers(0, R, (H, T)); J[:, rng.integers(T)] = rng.permutation(R)[:H]
    if how == "distinct": O[:], J = rng.integers(N), rng.permutation(R)[:H * T].reshape(H, T)
    if how == "hotrank":
        s = rng.integers(1, H); O[:] = np.array([rng.choice(G[(k + s) % H]) for k in range(H)])[:, None]; J = np.stack([rng.permutation(R)[:T] for g in G])
    I = R * O + J
    if how == "edge":
        C, Q = rng.integers(0, 2 * N, (H, T)), rng.permutation(T)
        C[:, Q[:2 * N]] = np.stack([rng.permutation(2 * N) for g in G]); C[:, Q[2 * N]] = rng.permutation(2 * N)[:H]
        I = R * (C // 2) + (R - 1) * (C % 2)
    return {"idx": np.stack([pack(I[K[r]], 16) for r in range(N)])}
def setup_inputs(rng):
    return dict({"tab": rng.standard_normal((N, 128, R), dtype=np.float32)}, **lists(rng, "uniform"))
def setup_inputs_away(rng):
    d = setup_inputs(rng); d.update(lists(rng, "away"))
    for k in ("tab",): d[k] = (d[k].astype(np.float32) * 1048576.0).astype(d[k].dtype)
    return d
def setup_inputs_distinct(rng):
    d = setup_inputs(rng); d.update(lists(rng, "distinct"))
    for k in ("tab",): d[k] = (d[k].astype(np.float32) * (1 / 1024.0)).astype(d[k].dtype)
    return d
def setup_inputs_edge(rng):
    d = setup_inputs(rng); d.update(lists(rng, "edge"))
    return d
def setup_inputs_home(rng):
    d = setup_inputs(rng); d.update(lists(rng, "home"))
    return d
def setup_inputs_hotrank(rng):
    d = setup_inputs(rng); d.update(lists(rng, "hotrank"))
    return d
def check_inputs(x):
    bad = []
    if x["idx"].min() < 0 or x["idx"].max() >= N * R: bad.append("idx out of range")
    if any((x["idx"][r] != x["idx"][s]).any() for r in range(N) for s in range(r) if HOST[r] == HOST[s]): bad.append("two ranks of one host hold different lists")
    return bad
def reference(tab, idx):
    A = np.concatenate(list(tab), axis=1)
    return {"y": np.stack([A[:, entries(idx[r])] for r in range(N)])}

@@ -1,0 +1,269 @@
+from concourse.bass import DstId, RemoteDMATransfer
+from concourse.mybir import AluOpType, ActivationFunctionType
+import comms_topo
+
+N, R, T_ENT = 6, 8192, 2048
+WORLD = 256
+Q = 4
+C = T_ENT // Q
+HC = C // 2
+OC = C // 16
+LC = T_ENT // 16
+PIECES, DEPTH = 8, 3
+OWNER_BITS = 65535 & ~(C - 1)
+SHIFT = (R // C).bit_length() - 1
+SLOTS = 5
+
+SCRATCH = {
+    "part": ("sbuf", [128, R], "float32"),
+    "lh": ("sbuf", [128, LC], "int32"),
+    "lo": ("sbuf", [128, LC], "int32"),
+    "th": ("sbuf", [128, LC], "int32"),
+    "to": ("sbuf", [128, LC], "int32"),
+    "gofh": ("sbuf", [128, LC], "uint16"),
+    "gofo": ("sbuf", [128, LC], "uint16"),
+    "pp": ("sbuf", [128, OC], "int32"),
+    "cc": ("sbuf", [128, OC], "int32"),
+    "pm": ("sbuf", [128, OC], "int32"),
+    "jj": ("sbuf", [128, OC], "int32"),
+    "ah": ("sbuf", [128, OC], "int32"),
+    "bh": ("sbuf", [128, OC], "int32"),
+    "ch": ("sbuf", [128, OC], "int32"),
+    "ao": ("sbuf", [128, OC], "int32"),
+    "bo": ("sbuf", [128, OC], "int32"),
+    "selh": ("sbuf", [128, OC], "uint16"),
+    "selo": ("sbuf", [128, OC], "uint16"),
+    "po": ("sbuf", [128, T_ENT], "float32"),
+    "ph": ("sbuf", [128, T_ENT], "float32"),
+    "wo": ("sbuf", [128, (SLOTS - 1) * C], "float32"),
+    "wh": ("sbuf", [128, SLOTS * C], "float32"),
+    "xo": ("sbuf", [128, C], "float32"),
+    "yb": ("sbuf", [128, T_ENT], "float32"),
+}
+SEMAPHORES = (["li", "io_", "vs", "lharr", "loarr", "okgh", "okgo", "oksh", "okso", "arro", "arrh", "arrx", "so", "sf", "ag",
+               "sent", "sty", "sta"]
+              + ["ld%d" % k for k in range(PIECES)] + ["go%d" % k for k in range(Q)] + ["gh%d" % k for k in range(Q)]
+              + ["ya%d" % k for k in range(Q)])
+
+
+def popcount(m):
+    return bin(m).count("1")
+
+
+def own_list_masks(q, full, lo, hi, n):
+    before_full = (q + 1) // 2
+    masks = [full] * min(before_full, n)
+    while len(masks) < n and len(masks) < before_full + 2:
+        masks.append(hi)
+    early = len(masks)
+    while len(masks) < n:
+        masks.append(lo)
+    return masks, early
+
+
+def rank_program(g, core, T, topo):
+    cores = list(T.cores)
+    hosts = sorted(set(topo.host(c) for c in cores))
+    group = {h: [c for c in cores if topo.host(c) == h] for h in hosts}
+    h = topo.host(core)
+    if h not in group:
+        return
+
+    def die_of(x):
+        a = group[x][0]
+        return [c for c in range(WORLD) if (topo.host(c), topo.chip(c), topo.die(c)) == (topo.host(a), topo.chip(a), topo.die(a))]
+    reducers = {x: die_of(x)[:Q] for x in hosts}
+    if core not in reducers[h]:
+        return
+    other = [x for x in hosts if x != h][0]
+    mine, red, far = group[h], reducers[h], reducers[other]
+    q = red.index(core)
+    rank = T.rank_of(core)
+    first, last = T.rank_of(mine[0]), T.rank_of(mine[-1])
+    base_h = max(first - 1, 0)
+    slot_x = 0 if first > 0 else last + 1 - base_h
+    peer = [c for c in red if c != core]
+    full = topo.mask(core, peer[0])
+    off = topo.mask(core, far[q])
+    hi = full & ~off
+
+    V, S, Y = g.vector, g.scalar, g.sync
+    A = AluOpType
+    COPY = ActivationFunctionType.Copy
+    sem = T.sem
+    sent = [0]
+
+    def send(dsts, out, src, rsem, mask):
+        ids = []
+        for d in dsts:
+            rid, pid = topo.addr(d, core)
+            ids.append(DstId(rid=rid, pnc=pid))
+        sent[0] += popcount(mask)
+        return RemoteDMATransfer(dst_ids=ids, dma_engine_mask=mask, remote_sem=rsem, srcs=[src], dsts=[out] * len(ids))
+
+    def write(d, out, src, rsem, mask):
+        rid, pid = topo.addr(d, core)
+        sent[0] += popcount(mask)
+        g.remote_dma(out_ap=out, in_ap=src, remote_sem=rsem, local_sem=sem.sent, pid=pid, routing_id=rid, dma_engine_mask=mask)
+
+    if rank is not None:
+        for k in range(8):
+            (S if k % 2 else Y).dma_start(T.lh[16 * k:16 * k + 16, :], T.idx[:]).then_inc(sem.li, 16)
+        rows = 128 // PIECES
+        for k in range(PIECES):
+            if k >= DEPTH:
+                Y.wait_ge(sem["ld%d" % (k - DEPTH)], 16)
+            Y.dma_start(T.part[rows * k:rows * (k + 1), :], T.tab[rows * k:rows * (k + 1), :]).then_inc(sem["ld%d" % k], 16)
+
+    def wait_list(e):
+        if rank is not None:
+            e.wait_ge(sem.li, 128)
+        else:
+            e.wait_ge(sem.lharr, popcount(hi))
+
+    g.iota(T.pp[:], [[0, OC]], 0, 1).then_inc(sem.io_, 1)
+    g.iota(T.cc[:], [[16, OC]], 0, 0).then_inc(sem.io_, 1)
+    if rank is not None:
+        p, n = mine.index(core), len(mine)
+        fars = far[p * Q // n:(p + 1) * Q // n]
+        bare = [c for c in red if c not in mine][p::n]
+        wait_list(g)
+        tr = [send(fars, T.lo[:], T.lh[:], sem.loarr, off)]
+        if bare:
+            tr.append(send(bare, T.lh[:], T.lh[:], sem.lharr, hi))
+        g.remote_dma_fused(tr, local_sem=sem.sent)
+
+    nv = [0]
+
+    def chained(ins):
+        nv[0] += 1
+        ins.then_inc(sem.vs, 1)
+        V.wait_ge(sem.vs, nv[0])
+
+    cols = slice(OC * q, OC * (q + 1))
+    V.wait_ge(sem.io_, 2)
+    chained(V.tensor_scalar(T.pm[:], T.pp[:], 15, None, A.bitwise_and))
+    chained(V.tensor_tensor(T.jj[:], T.pm[:], T.cc[:], A.add))
+    wait_list(V)
+    if rank is not None:
+        chained(V.tensor_scalar(T.th[:], T.lh[:], R - 1, None, A.bitwise_and))
+        V.tensor_copy(T.gofh[:], T.th[:]).then_inc(sem.okgh, 1)
+    chained(V.tensor_scalar(T.ah[:], T.lh[:, cols], SHIFT, OWNER_BITS, A.arith_shift_right, A.bitwise_and))
+    if first > 0:
+        chained(V.tensor_scalar(T.bh[:], T.ah[:], (first - 1) * C, -base_h * C, A.max, A.add))
+    else:
+        chained(V.tensor_scalar(T.bh[:], T.ah[:], (last + 1) * C, -base_h * C, A.min, A.add))
+    chained(V.tensor_tensor(T.ch[:], T.bh[:], T.jj[:], A.add))
+    V.tensor_copy(T.selh[:], T.ch[:]).then_inc(sem.oksh, 1)
+
+    V.wait_ge(sem.loarr, popcount(off))
+    if rank is not None:
+        chained(V.tensor_scalar(T.to[:], T.lo[:], R - 1, None, A.bitwise_and))
+        V.tensor_copy(T.gofo[:], T.to[:]).then_inc(sem.okgo, 1)
+        me_o, me_h = rank - first, rank - base_h
+
+    def gather(e, half, offs, buf, win, slot, tag):
+        for k in range(Q):
+            a = C * k + HC * half
+            out = buf[:, a:a + HC] if k != q else win[:, C * slot + HC * half:C * slot + HC * half + HC]
+            c0 = OC * k + (OC // 2) * half
+            src = T.part[:, 0:R].indirect(offs[:, c0:c0 + OC // 2])
+            ins = e.tensor_copy(out, src) if half == 0 else e.activation(out, src, COPY)
+            ins.then_inc(sem["%s%d" % (tag, k)], 1)
+
+    def pick_offsets_o():
+        chained(V.tensor_scalar(T.ao[:], T.lo[:, cols], SHIFT, OWNER_BITS, A.arith_shift_right, A.bitwise_and))
+        chained(V.tensor_tensor(T.bo[:], T.ao[:], T.jj[:], A.add))
+        if first > 0:
+            V.tensor_scalar(T.selo[:], T.bo[:], -first * C, 0, A.add, A.max).then_inc(sem.okso, 1)
+        else:
+            V.tensor_scalar(T.selo[:], T.bo[:], 0, (last + 1) * C - 1, A.add, A.min).then_inc(sem.okso, 1)
+
+    if rank is not None:
+        for e, half in ((V, 0), (S, 1)):
+            e.wait_ge(sem.okgo, 1)
+            for k in range(PIECES):
+                e.wait_ge(sem["ld%d" % k], 16)
+            gather(e, half, T.gofo, T.po, T.wo, me_o, "go")
+            if half == 0:
+                pick_offsets_o()
+            e.wait_ge(sem.okgh, 1)
+            gather(e, half, T.gofh, T.ph, T.wh, me_h, "gh")
+    else:
+        pick_offsets_o()
+
+    n_o = n_h = 0
+    for c in mine:
+        if c == core:
+            continue
+        cq = red.index(c)
+        f_c = topo.mask(c, core)
+        o_c = topo.mask(c, far[cq])
+        to = [k for k in range(Q) if k != cq]
+        masks, _early = own_list_masks(cq, f_c, o_c, f_c & ~o_c, len(to))
+        n_o += popcount(f_c)
+        n_h += popcount(masks[to.index(q)])
+
+    early = rest = ()
+    if rank is not None:
+        to = [k for k in range(Q) if k != q]
+        for k in to:
+            g.wait_ge(sem["go%d" % k], 2)
+            write(red[k], T.wo[:, C * me_o:C * (me_o + 1)], T.po[:, C * k:C * (k + 1)], sem.arro, full)
+        masks, ne = own_list_masks(q, full, off, hi, len(to))
+        early, rest = list(zip(to, masks))[:ne], list(zip(to, masks))[ne:]
+
+    def own_chunks(pairs):
+        for k, m in pairs:
+            g.wait_ge(sem["gh%d" % k], 2)
+            write(red[k], T.wh[:, C * me_h:C * (me_h + 1)], T.ph[:, C * k:C * (k + 1)], sem.arrh, m)
+    own_chunks(early)
+
+    wide_o, wide_h = len(mine) * C, (len(mine) + 1) * C
+    for e, half in ((V, 0), (S, 1)):
+        oc = slice(OC // 2 * half, OC // 2 * (half + 1))
+        e.wait_ge(sem.okso, 1)
+        if rank is not None:
+            e.wait_ge(sem["go%d" % q], 2)
+        e.wait_ge(sem.arro, n_o)
+        src, out = T.wo[:, 0:wide_o].indirect(T.selo[:, oc]), T.xo[:, HC * half:HC * (half + 1)]
+        ins = e.tensor_copy(out, src) if half == 0 else e.activation(out, src, COPY)
+        ins.then_inc(sem.so, 1)
+        e.wait_ge(sem.oksh, 1)
+        if rank is not None:
+            e.wait_ge(sem["gh%d" % q], 2)
+        e.wait_ge(sem.arrh, n_h)
+        e.wait_ge(sem.arrx, popcount(topo.mask(far[q], core)))
+        src = T.wh[:, 0:wide_h].indirect(T.selh[:, oc])
+        out = T.yb[:, C * q + HC * half:C * q + HC * (half + 1)]
+        ins = e.tensor_copy(out, src) if half == 0 else e.activation(out, src, COPY)
+        ins.then_inc(sem.sf, 1)
+
+    g.wait_ge(sem.so, 2)
+    far_base = max(T.rank_of(group[other][0]) - 1, 0)
+    far_first, far_last = T.rank_of(group[other][0]), T.rank_of(group[other][-1])
+    far_slot = 0 if far_first > 0 else far_last + 1 - far_base
+    write(far[q], T.wh[:, C * far_slot:C * (far_slot + 1)], T.xo[:], sem.arrx, off)
+    own_chunks(rest)
+
+    g.wait_ge(sem.sf, 2)
+    mycols = slice(C * q, C * (q + 1))
+    g.remote_dma_fused([send([c for c in mine if c != core], T.yb[:, mycols], T.yb[:, mycols], sem["ya%d" % q], full)],
+                       local_sem=sem.sent)
+    if rank is not None:
+        g.sem_inc(sem.ag, 1)
+        Y.wait_ge(sem.sf, 2)
+        Y.wait_ge(sem.ag, 1)
+        Y.dma_start(T.y[:, mycols], T.yb[:, mycols]).then_inc(sem.sty, 16)
+        ny = na = 0
+        for i, k in enumerate(k for k in range(Q) if k != q):
+            e, s = (S, sem.sta) if i != 1 else (Y, sem.sty)
+            e.wait_ge(sem["ya%d" % k], popcount(topo.mask(red[k], core)))
+            e.dma_start(T.y[:, C * k:C * (k + 1)], T.yb[:, C * k:C * (k + 1)]).then_inc(s, 16)
+            if i != 1:
+                na += 1
+            else:
+                ny += 1
+        Y.wait_ge(sem.sty, 16 * (ny + 1))
+        S.wait_ge(sem.sta, 16 * na)
+    g.wait_ge(sem.sent, sent[0])

@@ -5,6 +5,7 @@ import comms_topo
 N, R, T_ENT = 6, 8192, 2048
 WORLD = 256
 Q = 4
+NHELP = 2
 C = T_ENT // Q
 HC = C // 2
 OC = C // 16
@@ -12,53 +13,52 @@ LC = T_ENT // 16
 PIECES, DEPTH = 8, 3
 OWNER_BITS = 65535 & ~(C - 1)
 SHIFT = (R // C).bit_length() - 1
-SLOTS = 5
+MAXK = 2
+EARLY_FEW = 2
 
 SCRATCH = {
     "part": ("sbuf", [128, R], "float32"),
     "lh": ("sbuf", [128, LC], "int32"),
     "lo": ("sbuf", [128, LC], "int32"),
+    "dsrc": ("dram", [128, 8], "int32"),
+    "dlo": ("dram", [2, 128, 8], "int32"),
+    "dlh": ("dram", [2, 128, 8], "int32"),
     "th": ("sbuf", [128, LC], "int32"),
     "to": ("sbuf", [128, LC], "int32"),
     "gofh": ("sbuf", [128, LC], "uint16"),
     "gofo": ("sbuf", [128, LC], "uint16"),
-    "pp": ("sbuf", [128, OC], "int32"),
-    "cc": ("sbuf", [128, OC], "int32"),
-    "pm": ("sbuf", [128, OC], "int32"),
-    "jj": ("sbuf", [128, OC], "int32"),
-    "ah": ("sbuf", [128, OC], "int32"),
-    "bh": ("sbuf", [128, OC], "int32"),
-    "ch": ("sbuf", [128, OC], "int32"),
+    "pp": ("sbuf", [128, MAXK * OC], "int32"),
+    "cc": ("sbuf", [128, MAXK * OC], "int32"),
+    "pm": ("sbuf", [128, MAXK * OC], "int32"),
+    "jj": ("sbuf", [128, MAXK * OC], "int32"),
+    "ah": ("sbuf", [128, MAXK * OC], "int32"),
+    "bh": ("sbuf", [128, MAXK * OC], "int32"),
+    "ch": ("sbuf", [128, MAXK * OC], "int32"),
     "ao": ("sbuf", [128, OC], "int32"),
     "bo": ("sbuf", [128, OC], "int32"),
-    "selh": ("sbuf", [128, OC], "uint16"),
+    "selh": ("sbuf", [128, MAXK * OC], "uint16"),
+    "selm": ("sbuf", [128, MAXK * OC], "uint16"),
     "selo": ("sbuf", [128, OC], "uint16"),
     "po": ("sbuf", [128, T_ENT], "float32"),
     "ph": ("sbuf", [128, T_ENT], "float32"),
-    "wo": ("sbuf", [128, (SLOTS - 1) * C], "float32"),
-    "wh": ("sbuf", [128, SLOTS * C], "float32"),
+    "wo": ("sbuf", [128, Q * C], "float32"),
+    "wh": ("sbuf", [128, 3072], "float32"),
     "xo": ("sbuf", [128, C], "float32"),
     "yb": ("sbuf", [128, T_ENT], "float32"),
 }
-SEMAPHORES = (["li", "io_", "vs", "lharr", "loarr", "okgh", "okgo", "oksh", "okso", "arro", "arrh", "arrx", "so", "sf", "ag",
-               "sent", "sty", "sta"]
+SEMAPHORES = (["li", "lio", "ld", "io_", "vs", "loarr", "okgh", "okgo", "oksh", "okso", "sent", "sty", "sta", "arro", "so"]
               + ["ld%d" % k for k in range(PIECES)] + ["go%d" % k for k in range(Q)] + ["gh%d" % k for k in range(Q)]
-              + ["ya%d" % k for k in range(Q)])
+              + ["ya%d" % k for k in range(Q)]
+              + ["%s%d" % (s, i) for s in ("arrh", "arrx", "sf", "ag") for i in range(MAXK)])
 
 
 def popcount(m):
     return bin(m).count("1")
 
 
-def own_list_masks(q, full, lo, hi, n):
-    before_full = (q + 1) // 2
-    masks = [full] * min(before_full, n)
-    while len(masks) < n and len(masks) < before_full + 2:
-        masks.append(hi)
-    early = len(masks)
-    while len(masks) < n:
-        masks.append(lo)
-    return masks, early
+def halves(m):
+    bits = [1 << b for b in range(m.bit_length()) if m >> b & 1]
+    return sum(bits[:len(bits) // 2]), sum(bits[len(bits) // 2:])
 
 
 def rank_program(g, core, T, topo):
@@ -69,23 +69,39 @@ def rank_program(g, core, T, topo):
     if h not in group:
         return
 
-    def die_of(x):
-        a = group[x][0]
-        return [c for c in range(WORLD) if (topo.host(c), topo.chip(c), topo.die(c)) == (topo.host(a), topo.chip(a), topo.die(a))]
-    reducers = {x: die_of(x)[:Q] for x in hosts}
-    if core not in reducers[h]:
-        return
+    def helpers_of(grp):
+        a = grp[0]
+        return [c for c in range(WORLD) if (topo.host(c), topo.chip(c)) == (topo.host(a), topo.chip(a))
+                and topo.die(c) != topo.die(a)][:NHELP]
+
+    def own_reducers(grp):
+        return [grp[k * len(grp) // Q] for k in range(Q)]
     other = [x for x in hosts if x != h][0]
-    mine, red, far = group[h], reducers[h], reducers[other]
-    q = red.index(core)
+    mine, far = group[h], group[other]
+    help_, far_help = helpers_of(mine), helpers_of(far)
+    red, far_red = own_reducers(mine), own_reducers(far)
+    ored, far_ored = help_ + mine[NHELP - Q:], far_help + far[NHELP - Q:]
+    if core not in ored and core not in mine:
+        return
     rank = T.rank_of(core)
+    few = len(mine) < len(far)
+    qo = ored.index(core) if core in ored else None
+    ward = core if rank is not None else mine[help_.index(core)]
+    own = [k for k in range(Q) if red[k] == ward]
+    nk, w = len(own), len(own) * OC
     first, last = T.rank_of(mine[0]), T.rank_of(mine[-1])
     base_h = max(first - 1, 0)
-    slot_x = 0 if first > 0 else last + 1 - base_h
-    peer = [c for c in red if c != core]
-    full = topo.mask(core, peer[0])
-    off = topo.mask(core, far[q])
-    hi = full & ~off
+    win_o, win_h = len(mine) * C, (len(mine) + 1) * C
+    far_slot = 0 if T.rank_of(far[0]) > 0 else T.rank_of(far[-1]) + 1
+    far_win = (len(far) + 1) * C
+    off = topo.mask(core, far[0])
+
+    def engines(c):
+        f, lo = topo.mask(c, [x for x in mine if x != c][0]), topo.mask(c, far[0])
+        return f, lo, f & ~lo
+
+    def place(rd, k):
+        return [x for x in range(Q) if rd[x] == rd[k]].index(k)
 
     V, S, Y = g.vector, g.scalar, g.sync
     A = AluOpType
@@ -93,20 +109,22 @@ def rank_program(g, core, T, topo):
     sem = T.sem
     sent = [0]
 
-    def send(dsts, out, src, rsem, mask):
+    def transfer(dsts, outs, src, rsem, mask):
         ids = []
         for d in dsts:
             rid, pid = topo.addr(d, core)
             ids.append(DstId(rid=rid, pnc=pid))
         sent[0] += popcount(mask)
-        return RemoteDMATransfer(dst_ids=ids, dma_engine_mask=mask, remote_sem=rsem, srcs=[src], dsts=[out] * len(ids))
+        return RemoteDMATransfer(dst_ids=ids, dma_engine_mask=mask, remote_sem=rsem, srcs=[src], dsts=outs)
 
-    def write(d, out, src, rsem, mask):
-        rid, pid = topo.addr(d, core)
-        sent[0] += popcount(mask)
-        g.remote_dma(out_ap=out, in_ap=src, remote_sem=rsem, local_sem=sem.sent, pid=pid, routing_id=rid, dma_engine_mask=mask)
+    def fused(*transfers):
+        g.remote_dma_fused(list(transfers), local_sem=sem.sent)
 
+    n_list = 2 * popcount(topo.mask(far[0], core))
     if rank is not None:
+        p = mine.index(core)
+        half_list = p % 2
+        S.dma_start(T.dsrc[:], T.idx[8 * half_list:8 * half_list + 8, :]).then_inc(sem.ld, 16)
         for k in range(8):
             (S if k % 2 else Y).dma_start(T.lh[16 * k:16 * k + 16, :], T.idx[:]).then_inc(sem.li, 16)
         rows = 128 // PIECES
@@ -114,24 +132,24 @@ def rank_program(g, core, T, topo):
             if k >= DEPTH:
                 Y.wait_ge(sem["ld%d" % (k - DEPTH)], 16)
             Y.dma_start(T.part[rows * k:rows * (k + 1), :], T.tab[rows * k:rows * (k + 1), :]).then_inc(sem["ld%d" % k], 16)
+    else:
+        n_list += 2 * popcount(engines(mine[0])[2])
+        Y.wait_ge(sem.loarr, n_list)
+        for k in range(8):
+            Y.dma_start(T.lh[16 * k:16 * k + 16, :], T.dlh[:]).then_inc(sem.li, 16)
+    S.wait_ge(sem.loarr, n_list)
+    for k in range(8):
+        S.dma_start(T.lo[16 * k:16 * k + 16, :], T.dlo[:]).then_inc(sem.lio, 16)
 
-    def wait_list(e):
-        if rank is not None:
-            e.wait_ge(sem.li, 128)
-        else:
-            e.wait_ge(sem.lharr, popcount(hi))
-
-    g.iota(T.pp[:], [[0, OC]], 0, 1).then_inc(sem.io_, 1)
-    g.iota(T.cc[:], [[16, OC]], 0, 0).then_inc(sem.io_, 1)
+    g.iota(T.pp[:, 0:w], [[0, w]], 0, 1).then_inc(sem.io_, 1)
+    g.iota(T.cc[:, 0:w], [[0, nk], [16, OC]], 0, 0).then_inc(sem.io_, 1)
     if rank is not None:
-        p, n = mine.index(core), len(mine)
-        fars = far[p * Q // n:(p + 1) * Q // n]
-        bare = [c for c in red if c not in mine][p::n]
-        wait_list(g)
-        tr = [send(fars, T.lo[:], T.lh[:], sem.loarr, off)]
-        if bare:
-            tr.append(send(bare, T.lh[:], T.lh[:], sem.lharr, hi))
-        g.remote_dma_fused(tr, local_sem=sem.sent)
+        d = p * len(far) // len(mine)
+        dsts = far + far_help if few else [far[d], far_help[d]]
+        near = help_ if few else [help_[p * NHELP // len(mine)]]
+        g.wait_ge(sem.ld, 16)
+        fused(transfer(dsts, [T.dlo[half_list]] * len(dsts), T.dsrc[:], sem.loarr, off))
+        fused(transfer(near, [T.dlh[half_list]] * len(near), T.dsrc[:], sem.loarr, engines(core)[2]))
 
     nv = [0]
 
@@ -140,130 +158,154 @@ def rank_program(g, core, T, topo):
         ins.then_inc(sem.vs, 1)
         V.wait_ge(sem.vs, nv[0])
 
-    cols = slice(OC * q, OC * (q + 1))
-    V.wait_ge(sem.io_, 2)
-    chained(V.tensor_scalar(T.pm[:], T.pp[:], 15, None, A.bitwise_and))
-    chained(V.tensor_tensor(T.jj[:], T.pm[:], T.cc[:], A.add))
-    wait_list(V)
-    if rank is not None:
-        chained(V.tensor_scalar(T.th[:], T.lh[:], R - 1, None, A.bitwise_and))
-        V.tensor_copy(T.gofh[:], T.th[:]).then_inc(sem.okgh, 1)
-    chained(V.tensor_scalar(T.ah[:], T.lh[:, cols], SHIFT, OWNER_BITS, A.arith_shift_right, A.bitwise_and))
-    if first > 0:
-        chained(V.tensor_scalar(T.bh[:], T.ah[:], (first - 1) * C, -base_h * C, A.max, A.add))
-    else:
-        chained(V.tensor_scalar(T.bh[:], T.ah[:], (last + 1) * C, -base_h * C, A.min, A.add))
-    chained(V.tensor_tensor(T.ch[:], T.bh[:], T.jj[:], A.add))
-    V.tensor_copy(T.selh[:], T.ch[:]).then_inc(sem.oksh, 1)
-
-    V.wait_ge(sem.loarr, popcount(off))
-    if rank is not None:
-        chained(V.tensor_scalar(T.to[:], T.lo[:], R - 1, None, A.bitwise_and))
-        V.tensor_copy(T.gofo[:], T.to[:]).then_inc(sem.okgo, 1)
-        me_o, me_h = rank - first, rank - base_h
-
-    def gather(e, half, offs, buf, win, slot, tag):
-        for k in range(Q):
-            a = C * k + HC * half
-            out = buf[:, a:a + HC] if k != q else win[:, C * slot + HC * half:C * slot + HC * half + HC]
-            c0 = OC * k + (OC // 2) * half
-            src = T.part[:, 0:R].indirect(offs[:, c0:c0 + OC // 2])
-            ins = e.tensor_copy(out, src) if half == 0 else e.activation(out, src, COPY)
-            ins.then_inc(sem["%s%d" % (tag, k)], 1)
+    def pick_offsets_h(out):
+        lcols = slice(OC * own[0], OC * own[0] + w)
+        chained(V.tensor_scalar(T.ah[:, 0:w], T.lh[:, lcols], SHIFT, OWNER_BITS, A.arith_shift_right, A.bitwise_and))
+        if first > 0:
+            chained(V.tensor_scalar(T.bh[:, 0:w], T.ah[:, 0:w], (first - 1) * C, -base_h * C, A.max, A.add))
+        else:
+            chained(V.tensor_scalar(T.bh[:, 0:w], T.ah[:, 0:w], (last + 1) * C, -base_h * C, A.min, A.add))
+        chained(V.tensor_tensor(T.ch[:, 0:w], T.bh[:, 0:w], T.jj[:, 0:w], A.add))
+        V.tensor_copy(out[:, 0:w], T.ch[:, 0:w]).then_inc(sem.oksh, 1)
 
     def pick_offsets_o():
-        chained(V.tensor_scalar(T.ao[:], T.lo[:, cols], SHIFT, OWNER_BITS, A.arith_shift_right, A.bitwise_and))
-        chained(V.tensor_tensor(T.bo[:], T.ao[:], T.jj[:], A.add))
+        chained(V.tensor_scalar(T.ao[:], T.lo[:, OC * qo:OC * (qo + 1)], SHIFT, OWNER_BITS, A.arith_shift_right, A.bitwise_and))
+        chained(V.tensor_tensor(T.bo[:], T.ao[:], T.jj[:, 0:OC], A.add))
         if first > 0:
             V.tensor_scalar(T.selo[:], T.bo[:], -first * C, 0, A.add, A.max).then_inc(sem.okso, 1)
         else:
             V.tensor_scalar(T.selo[:], T.bo[:], 0, (last + 1) * C - 1, A.add, A.min).then_inc(sem.okso, 1)
 
-    if rank is not None:
-        for e, half in ((V, 0), (S, 1)):
-            e.wait_ge(sem.okgo, 1)
-            for k in range(PIECES):
-                e.wait_ge(sem["ld%d" % k], 16)
-            gather(e, half, T.gofo, T.po, T.wo, me_o, "go")
-            if half == 0:
-                pick_offsets_o()
-            e.wait_ge(sem.okgh, 1)
-            gather(e, half, T.gofh, T.ph, T.wh, me_h, "gh")
-    else:
-        pick_offsets_o()
+    def take(e, half, out, src, s):
+        ins = e.tensor_copy(out, src) if half == 0 else e.activation(out, src, COPY)
+        ins.then_inc(s, 1)
 
-    n_o = n_h = 0
-    for c in mine:
-        if c == core:
-            continue
-        cq = red.index(c)
-        f_c = topo.mask(c, core)
-        o_c = topo.mask(c, far[cq])
-        to = [k for k in range(Q) if k != cq]
-        masks, _early = own_list_masks(cq, f_c, o_c, f_c & ~o_c, len(to))
-        n_o += popcount(f_c)
-        n_h += popcount(masks[to.index(q)])
+    def o_plan(c):
+        f, lo, hi = engines(c)
+        to = [k for k in range(Q) if ored[k] != c]
+        return [[(to[0], f)], [(to[1], lo), (to[2], hi)]] + [[(k, f)] for k in to[3:]]
 
-    early = rest = ()
-    if rank is not None:
-        to = [k for k in range(Q) if k != q]
-        for k in to:
-            g.wait_ge(sem["go%d" % k], 2)
-            write(red[k], T.wo[:, C * me_o:C * (me_o + 1)], T.po[:, C * k:C * (k + 1)], sem.arro, full)
-        masks, ne = own_list_masks(q, full, off, hi, len(to))
-        early, rest = list(zip(to, masks))[:ne], list(zip(to, masks))[ne:]
+    def arriving(plans, k):
+        return sum(popcount(m) for calls in plans for call in calls for x, m in call if x == k)
 
-    def own_chunks(pairs):
-        for k, m in pairs:
-            g.wait_ge(sem["gh%d" % k], 2)
-            write(red[k], T.wh[:, C * me_h:C * (me_h + 1)], T.ph[:, C * k:C * (k + 1)], sem.arrh, m)
-    own_chunks(early)
-
-    wide_o, wide_h = len(mine) * C, (len(mine) + 1) * C
-    for e, half in ((V, 0), (S, 1)):
-        oc = slice(OC // 2 * half, OC // 2 * (half + 1))
+    def pick_o(e, half):
         e.wait_ge(sem.okso, 1)
         if rank is not None:
-            e.wait_ge(sem["go%d" % q], 2)
-        e.wait_ge(sem.arro, n_o)
-        src, out = T.wo[:, 0:wide_o].indirect(T.selo[:, oc]), T.xo[:, HC * half:HC * (half + 1)]
-        ins = e.tensor_copy(out, src) if half == 0 else e.activation(out, src, COPY)
-        ins.then_inc(sem.so, 1)
-        e.wait_ge(sem.oksh, 1)
-        if rank is not None:
-            e.wait_ge(sem["gh%d" % q], 2)
-        e.wait_ge(sem.arrh, n_h)
-        e.wait_ge(sem.arrx, popcount(topo.mask(far[q], core)))
-        src = T.wh[:, 0:wide_h].indirect(T.selh[:, oc])
-        out = T.yb[:, C * q + HC * half:C * q + HC * (half + 1)]
-        ins = e.tensor_copy(out, src) if half == 0 else e.activation(out, src, COPY)
-        ins.then_inc(sem.sf, 1)
+            e.wait_ge(sem["go%d" % qo], 2)
+        e.wait_ge(sem.arro, arriving([o_plan(c) for c in mine if c != core], qo))
+        oc = OC // 2 * half
+        take(e, half, T.xo[:, HC * half:HC * (half + 1)], T.wo[:, 0:win_o].indirect(T.selo[:, oc:oc + OC // 2]), sem.so)
 
-    g.wait_ge(sem.so, 2)
-    far_base = max(T.rank_of(group[other][0]) - 1, 0)
-    far_first, far_last = T.rank_of(group[other][0]), T.rank_of(group[other][-1])
-    far_slot = 0 if far_first > 0 else far_last + 1 - far_base
-    write(far[q], T.wh[:, C * far_slot:C * (far_slot + 1)], T.xo[:], sem.arrx, off)
-    own_chunks(rest)
+    def picked_to_far():
+        a = far_win * place(far_red, qo) + C * far_slot
+        g.wait_ge(sem.so, 2)
+        fused(transfer([far_red[qo]], [T.wh[:, a:a + C]], T.xo[:], sem["arrx%d" % place(far_red, qo)], off))
 
-    g.wait_ge(sem.sf, 2)
-    mycols = slice(C * q, C * (q + 1))
-    g.remote_dma_fused([send([c for c in mine if c != core], T.yb[:, mycols], T.yb[:, mycols], sem["ya%d" % q], full)],
-                       local_sem=sem.sent)
-    if rank is not None:
-        g.sem_inc(sem.ag, 1)
-        Y.wait_ge(sem.sf, 2)
-        Y.wait_ge(sem.ag, 1)
-        Y.dma_start(T.y[:, mycols], T.yb[:, mycols]).then_inc(sem.sty, 16)
-        ny = na = 0
-        for i, k in enumerate(k for k in range(Q) if k != q):
-            e, s = (S, sem.sta) if i != 1 else (Y, sem.sty)
-            e.wait_ge(sem["ya%d" % k], popcount(topo.mask(red[k], core)))
+    V.wait_ge(sem.io_, 2)
+    chained(V.tensor_scalar(T.pm[:, 0:w], T.pp[:, 0:w], 15, None, A.bitwise_and))
+    chained(V.tensor_tensor(T.jj[:, 0:w], T.pm[:, 0:w], T.cc[:, 0:w], A.add))
+    V.wait_ge(sem.li, 128)
+
+    if rank is None:
+        pick_offsets_h(T.selm)
+        V.wait_ge(sem.lio, 128)
+        pick_offsets_o()
+        g.wait_ge(sem.oksh, 1)
+        fused(transfer([ward], [T.selh[:, 0:w]], T.selm[:, 0:w], sem.oksh, off))
+        for e, half in ((V, 0), (S, 1)):
+            pick_o(e, half)
+        picked_to_far()
+        g.wait_ge(sem.sent, sent[0])
+        return
+
+    me_o, me_h = rank - first, rank - base_h
+    helped = p < len(help_)
+    chained(V.tensor_scalar(T.th[:], T.lh[:], R - 1, None, A.bitwise_and))
+    V.tensor_copy(T.gofh[:], T.th[:]).then_inc(sem.okgh, 1)
+    if not helped:
+        pick_offsets_h(T.selh)
+    V.wait_ge(sem.lio, 128)
+    chained(V.tensor_scalar(T.to[:], T.lo[:], R - 1, None, A.bitwise_and))
+    V.tensor_copy(T.gofo[:], T.to[:]).then_inc(sem.okgo, 1)
+
+    def gather(e, half, ks, offs, buf, landing, tag):
+        for k in ks:
+            b, a = landing.get(k, (buf, C * k))
+            c0 = OC * k + (OC // 2) * half
+            take(e, half, b[:, a + HC * half:a + HC * (half + 1)], T.part[:, 0:R].indirect(offs[:, c0:c0 + OC // 2]),
+                 sem["%s%d" % (tag, k)])
+
+    def own_plan(c):
+        f, lo, hi = engines(c)
+        h0, h1 = halves(hi)
+        to = [k for k in range(Q) if red[k] != c]
+        if few:
+            return [[(k, hi)] for k in to]
+        if c not in ored:
+            return [[(to[0], f)], [(to[1], lo), (to[2], hi)]]
+        if mine.index(c) == Q - 1:
+            return [[(to[0], lo), (to[1], hi)], [(to[2], hi)]]
+        return [[(to[0], f)], [(to[1], h0), (to[2], h1)]]
+
+    order_o = [k for k in range(Q) if k != qo] + ([] if qo is None else [qo])
+    order_h = [k for k in range(Q) if k not in own] + own
+    h_plans = [own_plan(c) for c in mine if c != core]
+    n_early = EARLY_FEW if few else Q
+    land_o = {} if qo is None else {qo: (T.wo, C * me_o)}
+    land_h = {k: (T.wh, win_h * i + C * me_h) for i, k in enumerate(own)}
+    n_sel = popcount(topo.mask(help_[0], far[0])) if helped else 1
+    for e, half in ((V, 0), (S, 1)):
+        e.wait_ge(sem.okgo, 1)
+        for k in range(PIECES):
+            e.wait_ge(sem["ld%d" % k], 16)
+        gather(e, half, order_o, T.gofo, T.po, land_o, "go")
+        if half == 0 and qo is not None:
+            pick_offsets_o()
+        e.wait_ge(sem.okgh, 1)
+        gather(e, half, order_h[:n_early], T.gofh, T.ph, land_h, "gh")
+        if qo is not None:
+            pick_o(e, half)
+        gather(e, half, order_h[n_early:], T.gofh, T.ph, land_h, "gh")
+        e.wait_ge(sem.oksh, n_sel)
+        for i, k in enumerate(own):
+            e.wait_ge(sem["gh%d" % k], 2)
+            e.wait_ge(sem["arrh%d" % i], arriving(h_plans, k))
+            e.wait_ge(sem["arrx%d" % i], popcount(topo.mask(far_ored[k], core)))
+            oc = OC * i + OC // 2 * half
+            take(e, half, T.yb[:, C * k + HC * half:C * k + HC * (half + 1)],
+                 T.wh[:, win_h * i:win_h * (i + 1)].indirect(T.selh[:, oc:oc + OC // 2]), sem["sf%d" % i])
+
+    for call in o_plan(core):
+        for k, m in call:
+            g.wait_ge(sem["go%d" % k], 2)
+        fused(*[transfer([ored[k]], [T.wo[:, C * me_o:C * (me_o + 1)]], T.po[:, C * k:C * (k + 1)], sem.arro, m)
+                for k, m in call])
+    for call in own_plan(core):
+        tr = []
+        for k, m in call:
+            a = win_h * place(red, k) + C * me_h
+            g.wait_ge(sem["gh%d" % k], 2)
+            tr.append(transfer([red[k]], [T.wh[:, a:a + C]], T.ph[:, C * k:C * (k + 1)], sem["arrh%d" % place(red, k)], m))
+        fused(*tr)
+    if qo is not None:
+        picked_to_far()
+
+    turn = mine[p + 1:] + mine[:p]
+    for i, k in enumerate(own):
+        cols = slice(C * k, C * (k + 1))
+        g.wait_ge(sem["sf%d" % i], 2)
+        fused(transfer(turn, [T.yb[:, cols]] * len(turn), T.yb[:, cols], sem["ya%d" % k], engines(core)[0]))
+        g.sem_inc(sem["ag%d" % i], 1)
+        Y.wait_ge(sem["sf%d" % i], 2)
+        Y.wait_ge(sem["ag%d" % i], 1)
+        Y.dma_start(T.y[:, cols], T.yb[:, cols]).then_inc(sem.sty, 16)
+    ny, na = nk, 0
+    for j, c in enumerate(reversed(turn)):
+        e, s = (Y, sem.sty) if j == 1 else (S, sem.sta)
+        for k in [x for x in range(Q) if red[x] == c]:
+            e.wait_ge(sem["ya%d" % k], popcount(topo.mask(c, core)))
             e.dma_start(T.y[:, C * k:C * (k + 1)], T.yb[:, C * k:C * (k + 1)]).then_inc(s, 16)
-            if i != 1:
-                na += 1
-            else:
-                ny += 1
-        Y.wait_ge(sem.sty, 16 * (ny + 1))
-        S.wait_ge(sem.sta, 16 * na)
+            ny, na = ny + int(j == 1), na + int(j != 1)
+    Y.wait_ge(sem.sty, 16 * ny)
+    S.wait_ge(sem.sta, 16 * na)
     g.wait_ge(sem.sent, sent[0])

from concourse.bass import DstId, RemoteDMATransfer
from concourse.mybir import AluOpType, ActivationFunctionType
import comms_topo

N, R, T_ENT = 6, 8192, 2048
WORLD = 256
Q = 4
NHELP = 2
C = T_ENT // Q
HC = C // 2
OC = C // 16
LC = T_ENT // 16
PIECES, DEPTH = 8, 3
OWNER_BITS = 65535 & ~(C - 1)
SHIFT = (R // C).bit_length() - 1
MAXK = 2
EARLY_FEW = 2

SCRATCH = {
    "part": ("sbuf", [128, R], "float32"),
    "lh": ("sbuf", [128, LC], "int32"),
    "lo": ("sbuf", [128, LC], "int32"),
    "dsrc": ("dram", [128, 8], "int32"),
    "dlo": ("dram", [2, 128, 8], "int32"),
    "dlh": ("dram", [2, 128, 8], "int32"),
    "th": ("sbuf", [128, LC], "int32"),
    "to": ("sbuf", [128, LC], "int32"),
    "gofh": ("sbuf", [128, LC], "uint16"),
    "gofo": ("sbuf", [128, LC], "uint16"),
    "pp": ("sbuf", [128, MAXK * OC], "int32"),
    "cc": ("sbuf", [128, MAXK * OC], "int32"),
    "pm": ("sbuf", [128, MAXK * OC], "int32"),
    "jj": ("sbuf", [128, MAXK * OC], "int32"),
    "ah": ("sbuf", [128, MAXK * OC], "int32"),
    "bh": ("sbuf", [128, MAXK * OC], "int32"),
    "ch": ("sbuf", [128, MAXK * OC], "int32"),
    "ao": ("sbuf", [128, OC], "int32"),
    "bo": ("sbuf", [128, OC], "int32"),
    "selh": ("sbuf", [128, MAXK * OC], "uint16"),
    "selm": ("sbuf", [128, MAXK * OC], "uint16"),
    "selo": ("sbuf", [128, OC], "uint16"),
    "po": ("sbuf", [128, T_ENT], "float32"),
    "ph": ("sbuf", [128, T_ENT], "float32"),
    "wo": ("sbuf", [128, Q * C], "float32"),
    "wh": ("sbuf", [128, 3072], "float32"),
    "xo": ("sbuf", [128, C], "float32"),
    "yb": ("sbuf", [128, T_ENT], "float32"),
}
SEMAPHORES = (["li", "lio", "ld", "io_", "vs", "loarr", "okgh", "okgo", "oksh", "okso", "sent", "sty", "sta", "arro", "so"]
              + ["ld%d" % k for k in range(PIECES)] + ["go%d" % k for k in range(Q)] + ["gh%d" % k for k in range(Q)]
              + ["ya%d" % k for k in range(Q)]
              + ["%s%d" % (s, i) for s in ("arrh", "arrx", "sf", "ag") for i in range(MAXK)])


def popcount(m):
    return bin(m).count("1")


def halves(m):
    bits = [1 << b for b in range(m.bit_length()) if m >> b & 1]
    return sum(bits[:len(bits) // 2]), sum(bits[len(bits) // 2:])


def rank_program(g, core, T, topo):
    cores = list(T.cores)
    hosts = sorted(set(topo.host(c) for c in cores))
    group = {h: [c for c in cores if topo.host(c) == h] for h in hosts}
    h = topo.host(core)
    if h not in group:
        return

    def helpers_of(grp):
        a = grp[0]
        return [c for c in range(WORLD) if (topo.host(c), topo.chip(c)) == (topo.host(a), topo.chip(a))
                and topo.die(c) != topo.die(a)][:NHELP]

    def own_reducers(grp):
        return [grp[k * len(grp) // Q] for k in range(Q)]
    other = [x for x in hosts if x != h][0]
    mine, far = group[h], group[other]
    help_, far_help = helpers_of(mine), helpers_of(far)
    red, far_red = own_reducers(mine), own_reducers(far)
    ored, far_ored = help_ + mine[NHELP - Q:], far_help + far[NHELP - Q:]
    if core not in ored and core not in mine:
        return
    rank = T.rank_of(core)
    few = len(mine) < len(far)
    qo = ored.index(core) if core in ored else None
    ward = core if rank is not None else mine[help_.index(core)]
    own = [k for k in range(Q) if red[k] == ward]
    nk, w = len(own), len(own) * OC
    first, last = T.rank_of(mine[0]), T.rank_of(mine[-1])
    base_h = max(first - 1, 0)
    win_o, win_h = len(mine) * C, (len(mine) + 1) * C
    far_slot = 0 if T.rank_of(far[0]) > 0 else T.rank_of(far[-1]) + 1
    far_win = (len(far) + 1) * C
    off = topo.mask(core, far[0])

    def engines(c):
        f, lo = topo.mask(c, [x for x in mine if x != c][0]), topo.mask(c, far[0])
        return f, lo, f & ~lo

    def place(rd, k):
        return [x for x in range(Q) if rd[x] == rd[k]].index(k)

    V, S, Y = g.vector, g.scalar, g.sync
    A = AluOpType
    COPY = ActivationFunctionType.Copy
    sem = T.sem
    sent = [0]

    def transfer(dsts, outs, src, rsem, mask):
        ids = []
        for d in dsts:
            rid, pid = topo.addr(d, core)
            ids.append(DstId(rid=rid, pnc=pid))
        sent[0] += popcount(mask)
        return RemoteDMATransfer(dst_ids=ids, dma_engine_mask=mask, remote_sem=rsem, srcs=[src], dsts=outs)

    def fused(*transfers):
        g.remote_dma_fused(list(transfers), local_sem=sem.sent)

    n_list = 2 * popcount(topo.mask(far[0], core))
    if rank is not None:
        p = mine.index(core)
        half_list = p % 2
        S.dma_start(T.dsrc[:], T.idx[8 * half_list:8 * half_list + 8, :]).then_inc(sem.ld, 16)
        for k in range(8):
            (S if k % 2 else Y).dma_start(T.lh[16 * k:16 * k + 16, :], T.idx[:]).then_inc(sem.li, 16)
        rows = 128 // PIECES
        for k in range(PIECES):
            if k >= DEPTH:
                Y.wait_ge(sem["ld%d" % (k - DEPTH)], 16)
            Y.dma_start(T.part[rows * k:rows * (k + 1), :], T.tab[rows * k:rows * (k + 1), :]).then_inc(sem["ld%d" % k], 16)
    else:
        n_list += 2 * popcount(engines(mine[0])[2])
        Y.wait_ge(sem.loarr, n_list)
        for k in range(8):
            Y.dma_start(T.lh[16 * k:16 * k + 16, :], T.dlh[:]).then_inc(sem.li, 16)
    S.wait_ge(sem.loarr, n_list)
    for k in range(8):
        S.dma_start(T.lo[16 * k:16 * k + 16, :], T.dlo[:]).then_inc(sem.lio, 16)

    g.iota(T.pp[:, 0:w], [[0, w]], 0, 1).then_inc(sem.io_, 1)
    g.iota(T.cc[:, 0:w], [[0, nk], [16, OC]], 0, 0).then_inc(sem.io_, 1)
    if rank is not None:
        d = p * len(far) // len(mine)
        dsts = far + far_help if few else [far[d], far_help[d]]
        near = help_ if few else [help_[p * NHELP // len(mine)]]
        g.wait_ge(sem.ld, 16)
        fused(transfer(dsts, [T.dlo[half_list]] * len(dsts), T.dsrc[:], sem.loarr, off))
        fused(transfer(near, [T.dlh[half_list]] * len(near), T.dsrc[:], sem.loarr, engines(core)[2]))

    nv = [0]

    def chained(ins):
        nv[0] += 1
        ins.then_inc(sem.vs, 1)
        V.wait_ge(sem.vs, nv[0])

    def pick_offsets_h(out):
        lcols = slice(OC * own[0], OC * own[0] + w)
        chained(V.tensor_scalar(T.ah[:, 0:w], T.lh[:, lcols], SHIFT, OWNER_BITS, A.arith_shift_right, A.bitwise_and))
        if first > 0:
            chained(V.tensor_scalar(T.bh[:, 0:w], T.ah[:, 0:w], (first - 1) * C, -base_h * C, A.max, A.add))
        else:
            chained(V.tensor_scalar(T.bh[:, 0:w], T.ah[:, 0:w], (last + 1) * C, -base_h * C, A.min, A.add))
        chained(V.tensor_tensor(T.ch[:, 0:w], T.bh[:, 0:w], T.jj[:, 0:w], A.add))
        V.tensor_copy(out[:, 0:w], T.ch[:, 0:w]).then_inc(sem.oksh, 1)

    def pick_offsets_o():
        chained(V.tensor_scalar(T.ao[:], T.lo[:, OC * qo:OC * (qo + 1)], SHIFT, OWNER_BITS, A.arith_shift_right, A.bitwise_and))
        chained(V.tensor_tensor(T.bo[:], T.ao[:], T.jj[:, 0:OC], A.add))
        if first > 0:
            V.tensor_scalar(T.selo[:], T.bo[:], -first * C, 0, A.add, A.max).then_inc(sem.okso, 1)
        else:
            V.tensor_scalar(T.selo[:], T.bo[:], 0, (last + 1) * C - 1, A.add, A.min).then_inc(sem.okso, 1)

    def take(e, half, out, src, s):
        ins = e.tensor_copy(out, src) if half == 0 else e.activation(out, src, COPY)
        ins.then_inc(s, 1)

    def o_plan(c):
        f, lo, hi = engines(c)
        to = [k for k in range(Q) if ored[k] != c]
        return [[(to[0], f)], [(to[1], lo), (to[2], hi)]] + [[(k, f)] for k in to[3:]]

    def arriving(plans, k):
        return sum(popcount(m) for calls in plans for call in calls for x, m in call if x == k)

    def pick_o(e, half):
        e.wait_ge(sem.okso, 1)
        if rank is not None:
            e.wait_ge(sem["go%d" % qo], 2)
        e.wait_ge(sem.arro, arriving([o_plan(c) for c in mine if c != core], qo))
        oc = OC // 2 * half
        take(e, half, T.xo[:, HC * half:HC * (half + 1)], T.wo[:, 0:win_o].indirect(T.selo[:, oc:oc + OC // 2]), sem.so)

    def picked_to_far():
        a = far_win * place(far_red, qo) + C * far_slot
        g.wait_ge(sem.so, 2)
        fused(transfer([far_red[qo]], [T.wh[:, a:a + C]], T.xo[:], sem["arrx%d" % place(far_red, qo)], off))

    V.wait_ge(sem.io_, 2)
    chained(V.tensor_scalar(T.pm[:, 0:w], T.pp[:, 0:w], 15, None, A.bitwise_and))
    chained(V.tensor_tensor(T.jj[:, 0:w], T.pm[:, 0:w], T.cc[:, 0:w], A.add))
    V.wait_ge(sem.li, 128)

    if rank is None:
        pick_offsets_h(T.selm)
        V.wait_ge(sem.lio, 128)
        pick_offsets_o()
        g.wait_ge(sem.oksh, 1)
        fused(transfer([ward], [T.selh[:, 0:w]], T.selm[:, 0:w], sem.oksh, off))
        for e, half in ((V, 0), (S, 1)):
            pick_o(e, half)
        picked_to_far()
        g.wait_ge(sem.sent, sent[0])
        return

    me_o, me_h = rank - first, rank - base_h
    helped = p < len(help_)
    chained(V.tensor_scalar(T.th[:], T.lh[:], R - 1, None, A.bitwise_and))
    V.tensor_copy(T.gofh[:], T.th[:]).then_inc(sem.okgh, 1)
    if not helped:
        pick_offsets_h(T.selh)
    V.wait_ge(sem.lio, 128)
    chained(V.tensor_scalar(T.to[:], T.lo[:], R - 1, None, A.bitwise_and))
    V.tensor_copy(T.gofo[:], T.to[:]).then_inc(sem.okgo, 1)

    def gather(e, half, ks, offs, buf, landing, tag):
        for k in ks:
            b, a = landing.get(k, (buf, C * k))
            c0 = OC * k + (OC // 2) * half
            take(e, half, b[:, a + HC * half:a + HC * (half + 1)], T.part[:, 0:R].indirect(offs[:, c0:c0 + OC // 2]),
                 sem["%s%d" % (tag, k)])

    def own_plan(c):
        f, lo, hi = engines(c)
        h0, h1 = halves(hi)
        to = [k for k in range(Q) if red[k] != c]
        if few:
            return [[(k, hi)] for k in to]
        if c not in ored:
            return [[(to[0], f)], [(to[1], lo), (to[2], hi)]]
        if mine.index(c) == Q - 1:
            return [[(to[0], lo), (to[1], hi)], [(to[2], hi)]]
        return [[(to[0], f)], [(to[1], h0), (to[2], h1)]]

    order_o = [k for k in range(Q) if k != qo] + ([] if qo is None else [qo])
    order_h = [k for k in range(Q) if k not in own] + own
    h_plans = [own_plan(c) for c in mine if c != core]
    n_early = EARLY_FEW if few else Q
    land_o = {} if qo is None else {qo: (T.wo, C * me_o)}
    land_h = {k: (T.wh, win_h * i + C * me_h) for i, k in enumerate(own)}
    n_sel = popcount(topo.mask(help_[0], far[0])) if helped else 1
    for e, half in ((V, 0), (S, 1)):
        e.wait_ge(sem.okgo, 1)
        for k in range(PIECES):
            e.wait_ge(sem["ld%d" % k], 16)
        gather(e, half, order_o, T.gofo, T.po, land_o, "go")
        if half == 0 and qo is not None:
            pick_offsets_o()
        e.wait_ge(sem.okgh, 1)
        gather(e, half, order_h[:n_early], T.gofh, T.ph, land_h, "gh")
        if qo is not None:
            pick_o(e, half)
        gather(e, half, order_h[n_early:], T.gofh, T.ph, land_h, "gh")
        e.wait_ge(sem.oksh, n_sel)
        for i, k in enumerate(own):
            e.wait_ge(sem["gh%d" % k], 2)
            e.wait_ge(sem["arrh%d" % i], arriving(h_plans, k))
            e.wait_ge(sem["arrx%d" % i], popcount(topo.mask(far_ored[k], core)))
            oc = OC * i + OC // 2 * half
            take(e, half, T.yb[:, C * k + HC * half:C * k + HC * (half + 1)],
                 T.wh[:, win_h * i:win_h * (i + 1)].indirect(T.selh[:, oc:oc + OC // 2]), sem["sf%d" % i])

    for call in o_plan(core):
        for k, m in call:
            g.wait_ge(sem["go%d" % k], 2)
        fused(*[transfer([ored[k]], [T.wo[:, C * me_o:C * (me_o + 1)]], T.po[:, C * k:C * (k + 1)], sem.arro, m)
                for k, m in call])
    for call in own_plan(core):
        tr = []
        for k, m in call:
            a = win_h * place(red, k) + C * me_h
            g.wait_ge(sem["gh%d" % k], 2)
            tr.append(transfer([red[k]], [T.wh[:, a:a + C]], T.ph[:, C * k:C * (k + 1)], sem["arrh%d" % place(red, k)], m))
        fused(*tr)
    if qo is not None:
        picked_to_far()

    turn = mine[p + 1:] + mine[:p]
    for i, k in enumerate(own):
        cols = slice(C * k, C * (k + 1))
        g.wait_ge(sem["sf%d" % i], 2)
        fused(transfer(turn, [T.yb[:, cols]] * len(turn), T.yb[:, cols], sem["ya%d" % k], engines(core)[0]))
        g.sem_inc(sem["ag%d" % i], 1)
        Y.wait_ge(sem["sf%d" % i], 2)
        Y.wait_ge(sem["ag%d" % i], 1)
        Y.dma_start(T.y[:, cols], T.yb[:, cols]).then_inc(sem.sty, 16)
    ny, na = nk, 0
    for j, c in enumerate(reversed(turn)):
        e, s = (Y, sem.sty) if j == 1 else (S, sem.sta)
        for k in [x for x in range(Q) if red[x] == c]:
            e.wait_ge(sem["ya%d" % k], popcount(topo.mask(c, core)))
            e.dma_start(T.y[:, C * k:C * (k + 1)], T.yb[:, C * k:C * (k + 1)]).then_inc(s, 16)
            ny, na = ny + int(j == 1), na + int(j != 1)
    Y.wait_ge(sem.sty, 16 * ny)
    S.wait_ge(sem.sta, 16 * na)
    g.wait_ge(sem.sent, sent[0])
